import numpy as np, ml_dtypes
CORES = [2,6,10,14,18,22]
N = 6
KT, F = 4, 256
def setup_inputs(rng):
    return {"a": rng.standard_normal((N, 128, KT * 128), dtype=np.float32).astype(ml_dtypes.bfloat16), "w": rng.standard_normal((N, 128, KT * F), dtype=np.float32).astype(ml_dtypes.bfloat16)}
def reference(a, w):
    A, W = a.astype(np.float64), w.astype(np.float64)
    y = np.zeros((N, 128, N * F))
    for r in range(N):
        for j in range(N):
            for t in range(KT):
                y[r][:, F * j:F * j + F] += A[j][:, 128 * t:128 * t + 128].T @ W[r][:, F * t:F * t + F]
    return {"y": y.astype(ml_dtypes.bfloat16 if a.dtype != np.float64 else np.float64)}

@@ -1,0 +1,178 @@
+from concourse.bass import DstId, RemoteDMATransfer
+
+N, KT, F, P = 6, 4, 256, 128
+AW = KT * P
+
+ROUNDS = ((("sib",), ("nX",)), (("nY",), ("fY",)))
+FORWARD = {"nX": ("fX",)}
+HOP = 2.5
+
+SCRATCH = {
+    "ag": ("sbuf", [P, N * AW], "bfloat16"),
+    "wsb": ("sbuf", [P, KT * F], "bfloat16"),
+    "ysb": ("sbuf", [P, N * F], "bfloat16"),
+}
+for _j in range(N):
+    SCRATCH["p%d" % _j] = ("psum", [P, 512], "float32")
+
+SEMAPHORES = (["la", "lw", "sent", "st0", "st1"] + ["arr%d" % j for j in range(N)]
+              + ["mm%d" % j for j in range(N)] + ["cp%d" % j for j in range(N)])
+
+
+def _bits(mask):
+    return [1 << b for b in range(mask.bit_length()) if (mask >> b) & 1]
+
+
+def _share(pool, n):
+    base = 1
+    while base * 2 * n <= len(pool):
+        base *= 2
+    sizes = [base] * n
+    left = len(pool) - base * n
+    for i in range(n):
+        if left >= sizes[i]:
+            left -= sizes[i]
+            sizes[i] *= 2
+    out, at = [], 0
+    for s in sizes:
+        out.append((sum(pool[at:at + s]), s))
+        at += s
+    return out
+
+
+def _roles(T, topo, c):
+    ranks = list(T.cores)
+    chips = []
+    for r in ranks:
+        if topo.chip(r) not in chips:
+            chips.append(topo.chip(r))
+    k = chips.index(topo.chip(c))
+
+    def on(ch, same_die):
+        return [r for r in ranks if topo.chip(r) == ch and r != c and (topo.die(r) == topo.die(c)) == same_die][0]
+
+    X, Y = chips[(k - 1) % len(chips)], chips[(k + 1) % len(chips)]
+    return {"sib": on(topo.chip(c), False), "nX": on(X, True), "fX": on(X, False),
+            "nY": on(Y, True), "fY": on(Y, False)}
+
+
+def _masks(topo, src, groups):
+    off = [i for i, d in enumerate(groups) if topo.chip(d[0]) != topo.chip(src)]
+    on = [i for i, d in enumerate(groups) if topo.chip(d[0]) == topo.chip(src)]
+    pool_off = _bits(topo.mask(src, groups[off[0]][0])) if off else []
+    pool_on = [b for b in _bits(topo.mask(src, groups[on[0]][0])) if b not in pool_off] if on else []
+    res = [None] * len(groups)
+    for idx, pool in ((off, pool_off), (on, pool_on)):
+        if idx:
+            for i, m in zip(idx, _share(pool, len(idx))):
+                res[i] = m
+    return res
+
+
+def _plan(T, topo):
+    calls = {}
+    arrive = {}
+
+    def add(src, eta0, wait, groups, j, etas):
+        tr = []
+        for (mask, n), dsts, es in zip(_masks(topo, src, groups), groups, etas):
+            tr.append((mask, n, dsts, j))
+            for d, e in zip(dsts, es):
+                assert topo.may_write(src, d)
+                arrive.setdefault(d, {})[j] = (n, e)
+        calls.setdefault(src, []).append((eta0, wait, tr))
+
+    for c in T.cores:
+        j, role, cnt = T.rank_of(c), _roles(T, topo, c), 0
+        for rnd in ROUNDS:
+            groups, etas = [], []
+            for g in rnd:
+                groups.append([role[x] for x in g])
+                es = []
+                for x in g:
+                    if x == "sib":
+                        es.append(0.5)
+                    else:
+                        cnt += 1
+                        es.append(float(cnt))
+                etas.append(es)
+            add(c, 0.0, None, groups, j, etas)
+    for c in T.cores:
+        j, role = T.rank_of(c), _roles(T, topo, c)
+        for x, to in FORWARD.items():
+            src = role[x]
+            e = arrive[src][j][1]
+            add(src, e, j, [[role[y]] for y in to], j, [[e + HOP] for y in to])
+    for c in calls:
+        calls[c].sort(key=lambda t: t[0])
+    return calls, arrive
+
+
+def rank_program(g, core, T, topo):
+    calls, arrive = _plan(T, topo)
+    rank = T.rank_of(core)
+    mine = calls.get(core, [])
+    if rank is None and not mine:
+        return
+    sem = T.sem
+    got = arrive.get(core, {})
+
+    if rank is not None:
+        g.sync.dma_start(T.ag[:, rank * AW:(rank + 1) * AW], T.a[:]).then_inc(sem.la, 16)
+        g.sync.dma_start(T.wsb[:], T.w[:]).then_inc(sem.lw, 16)
+
+    sent = 0
+    for _, wait, tr in mine:
+        if wait is None:
+            g.wait_ge(sem.la, 16)
+        else:
+            g.wait_ge(sem["arr%d" % wait], got[wait][0])
+        ts = []
+        for mask, n, dsts, j in tr:
+            ap = T.ag[:, j * AW:(j + 1) * AW]
+            ids = [DstId(rid=topo.addr(d)[0], pnc=topo.addr(d)[1]) for d in dsts]
+            ts.append(RemoteDMATransfer(dst_ids=ids, dma_engine_mask=mask, remote_sem=sem["arr%d" % j],
+                                        srcs=[ap], dsts=[ap for d in dsts]))
+            sent += n
+        g.remote_dma_fused(ts, local_sem=sem.sent)
+    if sent:
+        g.wait_ge(sem.sent, sent)
+    if rank is None:
+        return
+
+    order = [rank] + sorted(got, key=lambda j: (got[j][1], j))
+    g.tensor.wait_ge(sem.lw, 16)
+    for j in order:
+        if j == rank:
+            g.tensor.wait_ge(sem.la, 16)
+        else:
+            g.tensor.wait_ge(sem["arr%d" % j], got[j][0])
+        for t in range(KT):
+            mm = g.tensor.matmul(T["p%d" % j][:, 0:F], T.ag[:, j * AW + t * P:j * AW + (t + 1) * P],
+                                 T.wsb[:, t * F:(t + 1) * F], t == 0, t == KT - 1)
+        mm.then_inc(sem["mm%d" % j], 1)
+
+    for j in order:
+        g.vector.wait_ge(sem["mm%d" % j], 1)
+        g.vector.tensor_copy(T.ysb[:, j * F:(j + 1) * F], T["p%d" % j][:, 0:F]).then_inc(sem["cp%d" % j], 1)
+
+    groups, i = [], 0
+    while i < N:
+        if i + 2 < N and abs(order[i] - order[i + 1]) == 1:
+            groups.append((order[i], order[i + 1]))
+            i += 2
+        else:
+            groups.append((order[i],))
+            i += 1
+    queues = ((g.scalar, sem.st0), (g.sync, sem.st1))
+    count = [0, 0]
+    for k, grp in enumerate(groups):
+        q, s = queues[k % 2]
+        for j in grp:
+            q.wait_ge(sem["cp%d" % j], 1)
+        lo, hi = min(grp) * F, (max(grp) + 1) * F
+        q.dma_start(T.y[:, lo:hi], T.ysb[:, lo:hi]).then_inc(s, 16)
+        count[k % 2] += 16
+    for k in range(2):
+        if count[k]:
+            queues[k][0].wait_ge(queues[k][1], count[k])

@@ -3,7 +3,7 @@ from concourse.bass import DstId, RemoteDMATransfer
 N, KT, F, P = 6, 4, 256, 128
 AW = KT * P
 
-ROUNDS = ((("sib",), ("nX",)), (("nY",), ("fY",)))
+ROUNDS = ((("sib",), ("nX",)), (("nY",),), (("fY",),))
 FORWARD = {"nX": ("fX",)}
 HOP = 2.5
 

@@ -3,9 +3,9 @@ from concourse.bass import DstId, RemoteDMATransfer
 N, KT, F, P = 6, 4, 256, 128
 AW = KT * P
 
-ROUNDS = ((("sib",), ("nX",)), (("nY",),), (("fY",),))
+ROUNDS = ((("sib",), ("nX", "nY", "fY")),)
 FORWARD = {"nX": ("fX",)}
-HOP = 2.5
+HOP = 1.5
 
 SCRATCH = {
     "ag": ("sbuf", [P, N * AW], "bfloat16"),
@@ -56,10 +56,11 @@ def _roles(T, topo, c):
             "nY": on(Y, True), "fY": on(Y, False)}
 
 
-def _masks(topo, src, groups):
+def _masks(T, topo, src, groups):
+    away = [r for r in T.cores if topo.chip(r) != topo.chip(src)][0]
+    pool_off = _bits(topo.mask(src, away))
     off = [i for i, d in enumerate(groups) if topo.chip(d[0]) != topo.chip(src)]
     on = [i for i, d in enumerate(groups) if topo.chip(d[0]) == topo.chip(src)]
-    pool_off = _bits(topo.mask(src, groups[off[0]][0])) if off else []
     pool_on = [b for b in _bits(topo.mask(src, groups[on[0]][0])) if b not in pool_off] if on else []
     res = [None] * len(groups)
     for idx, pool in ((off, pool_off), (on, pool_on)):
@@ -75,7 +76,7 @@ def _plan(T, topo):
 
     def add(src, eta0, wait, groups, j, etas):
         tr = []
-        for (mask, n), dsts, es in zip(_masks(topo, src, groups), groups, etas):
+        for (mask, n), dsts, es in zip(_masks(T, topo, src, groups), groups, etas):
             tr.append((mask, n, dsts, j))
             for d, e in zip(dsts, es):
                 assert topo.may_write(src, d)

from concourse.bass import DstId, RemoteDMATransfer

N, KT, F, P = 6, 4, 256, 128
AW = KT * P

ROUNDS = ((("sib",), ("nX", "nY", "fY")),)
FORWARD = {"nX": ("fX",)}
HOP = 1.5

SCRATCH = {
    "ag": ("sbuf", [P, N * AW], "bfloat16"),
    "wsb": ("sbuf", [P, KT * F], "bfloat16"),
    "ysb": ("sbuf", [P, N * F], "bfloat16"),
}
for _j in range(N):
    SCRATCH["p%d" % _j] = ("psum", [P, 512], "float32")

SEMAPHORES = (["la", "lw", "sent", "st0", "st1"] + ["arr%d" % j for j in range(N)]
              + ["mm%d" % j for j in range(N)] + ["cp%d" % j for j in range(N)])


def _bits(mask):
    return [1 << b for b in range(mask.bit_length()) if (mask >> b) & 1]


def _share(pool, n):
    base = 1
    while base * 2 * n <= len(pool):
        base *= 2
    sizes = [base] * n
    left = len(pool) - base * n
    for i in range(n):
        if left >= sizes[i]:
            left -= sizes[i]
            sizes[i] *= 2
    out, at = [], 0
    for s in sizes:
        out.append((sum(pool[at:at + s]), s))
        at += s
    return out


def _roles(T, topo, c):
    ranks = list(T.cores)
    chips = []
    for r in ranks:
        if topo.chip(r) not in chips:
            chips.append(topo.chip(r))
    k = chips.index(topo.chip(c))

    def on(ch, same_die):
        return [r for r in ranks if topo.chip(r) == ch and r != c and (topo.die(r) == topo.die(c)) == same_die][0]

    X, Y = chips[(k - 1) % len(chips)], chips[(k + 1) % len(chips)]
    return {"sib": on(topo.chip(c), False), "nX": on(X, True), "fX": on(X, False),
            "nY": on(Y, True), "fY": on(Y, False)}


def _masks(T, topo, src, groups):
    away = [r for r in T.cores if topo.chip(r) != topo.chip(src)][0]
    pool_off = _bits(topo.mask(src, away))
    off = [i for i, d in enumerate(groups) if topo.chip(d[0]) != topo.chip(src)]
    on = [i for i, d in enumerate(groups) if topo.chip(d[0]) == topo.chip(src)]
    pool_on = [b for b in _bits(topo.mask(src, groups[on[0]][0])) if b not in pool_off] if on else []
    res = [None] * len(groups)
    for idx, pool in ((off, pool_off), (on, pool_on)):
        if idx:
            for i, m in zip(idx, _share(pool, len(idx))):
                res[i] = m
    return res


def _plan(T, topo):
    calls = {}
    arrive = {}

    def add(src, eta0, wait, groups, j, etas):
        tr = []
        for (mask, n), dsts, es in zip(_masks(T, topo, src, groups), groups, etas):
            tr.append((mask, n, dsts, j))
            for d, e in zip(dsts, es):
                assert topo.may_write(src, d)
                arrive.setdefault(d, {})[j] = (n, e)
        calls.setdefault(src, []).append((eta0, wait, tr))

    for c in T.cores:
        j, role, cnt = T.rank_of(c), _roles(T, topo, c), 0
        for rnd in ROUNDS:
            groups, etas = [], []
            for g in rnd:
                groups.append([role[x] for x in g])
                es = []
                for x in g:
                    if x == "sib":
                        es.append(0.5)
                    else:
                        cnt += 1
                        es.append(float(cnt))
                etas.append(es)
            add(c, 0.0, None, groups, j, etas)
    for c in T.cores:
        j, role = T.rank_of(c), _roles(T, topo, c)
        for x, to in FORWARD.items():
            src = role[x]
            e = arrive[src][j][1]
            add(src, e, j, [[role[y]] for y in to], j, [[e + HOP] for y in to])
    for c in calls:
        calls[c].sort(key=lambda t: t[0])
    return calls, arrive


def rank_program(g, core, T, topo):
    calls, arrive = _plan(T, topo)
    rank = T.rank_of(core)
    mine = calls.get(core, [])
    if rank is None and not mine:
        return
    sem = T.sem
    got = arrive.get(core, {})

    if rank is not None:
        g.sync.dma_start(T.ag[:, rank * AW:(rank + 1) * AW], T.a[:]).then_inc(sem.la, 16)
        g.sync.dma_start(T.wsb[:], T.w[:]).then_inc(sem.lw, 16)

    sent = 0
    for _, wait, tr in mine:
        if wait is None:
            g.wait_ge(sem.la, 16)
        else:
            g.wait_ge(sem["arr%d" % wait], got[wait][0])
        ts = []
        for mask, n, dsts, j in tr:
            ap = T.ag[:, j * AW:(j + 1) * AW]
            ids = [DstId(rid=topo.addr(d)[0], pnc=topo.addr(d)[1]) for d in dsts]
            ts.append(RemoteDMATransfer(dst_ids=ids, dma_engine_mask=mask, remote_sem=sem["arr%d" % j],
                                        srcs=[ap], dsts=[ap for d in dsts]))
            sent += n
        g.remote_dma_fused(ts, local_sem=sem.sent)
    if sent:
        g.wait_ge(sem.sent, sent)
    if rank is None:
        return

    order = [rank] + sorted(got, key=lambda j: (got[j][1], j))
    g.tensor.wait_ge(sem.lw, 16)
    for j in order:
        if j == rank:
            g.tensor.wait_ge(sem.la, 16)
        else:
            g.tensor.wait_ge(sem["arr%d" % j], got[j][0])
        for t in range(KT):
            mm = g.tensor.matmul(T["p%d" % j][:, 0:F], T.ag[:, j * AW + t * P:j * AW + (t + 1) * P],
                                 T.wsb[:, t * F:(t + 1) * F], t == 0, t == KT - 1)
        mm.then_inc(sem["mm%d" % j], 1)

    for j in order:
        g.vector.wait_ge(sem["mm%d" % j], 1)
        g.vector.tensor_copy(T.ysb[:, j * F:(j + 1) * F], T["p%d" % j][:, 0:F]).then_inc(sem["cp%d" % j], 1)

    groups, i = [], 0
    while i < N:
        if i + 2 < N and abs(order[i] - order[i + 1]) == 1:
            groups.append((order[i], order[i + 1]))
            i += 2
        else:
            groups.append((order[i],))
            i += 1
    queues = ((g.scalar, sem.st0), (g.sync, sem.st1))
    count = [0, 0]
    for k, grp in enumerate(groups):
        q, s = queues[k % 2]
        for j in grp:
            q.wait_ge(sem["cp%d" % j], 1)
        lo, hi = min(grp) * F, (max(grp) + 1) * F
        q.dma_start(T.y[:, lo:hi], T.ysb[:, lo:hi]).then_inc(s, 16)
        count[k % 2] += 16
    for k in range(2):
        if count[k]:
            queues[k][0].wait_ge(queues[k][1], count[k])
